import numpy as np
import ml_dtypes


def mxq(x, axis, fmt="e4m3"):
    dtype, down = {"e4m3": (ml_dtypes.float8_e4m3fn, 7), "e5m2": (ml_dtypes.float8_e5m2, 14)}[fmt]
    v = np.moveaxis(np.asarray(x, np.float32).astype(ml_dtypes.bfloat16).astype(np.float64), axis, -1)
    blocks = v.reshape(v.shape[:-1] + (-1, 32))
    amax = np.abs(blocks).max(-1, keepdims=True)
    byte = np.maximum(np.where(amax > 0, np.frexp(amax)[1] - 1 + 127, 0) - down, 1)
    scale = np.exp2(byte - 127.0)
    codes = (blocks / scale).astype(np.float32).astype(dtype).astype(np.float64)
    return np.moveaxis((codes * scale).reshape(v.shape), -1, axis)


WIDE = False


def mx_kscale(k):
    if not WIDE:
        return np.ones(k)
    levels = np.array([30, -30])
    if k % 512:
        return np.exp2(np.random.permutation(np.resize(levels, k // 32))).repeat(32)
    a = np.empty((k // 512, 16))
    for p in range(k // 512):
        a[p, :8] = np.random.permutation(np.resize(levels, 8))
        for g in range(8):
            far = levels[np.abs(levels - a[p, g]) >= 10]
            a[p, g + 8] = far[np.random.randint(len(far))]
    return np.exp2(a.ravel()).repeat(32)


def f64(x):
    return np.asarray(x).astype(np.float64)


def striped(idx):
    return np.tile(np.asarray(idx).reshape(-1, 16).T, (8, 1)).astype(np.uint16)


def unstriped(offs):
    return offs[:16].T.reshape(-1).astype(np.int64)


E2M1 = np.array([0.0, 0.5, 1.0, 1.5, 2.0, 3.0, 4.0, 6.0, -0.0, -0.5, -1.0, -1.5, -2.0, -3.0, -4.0, -6.0])


def pack_weight(w, fmt):
    k, n = w.shape
    w = f64(np.asarray(w, np.float32).astype(ml_dtypes.bfloat16)).reshape(k // 32, 32, n)
    amax = np.abs(w).max(1)
    if fmt == "e4m3":
        byte = np.frexp(amax)[1] - 1 + 127 - 7
    else:
        mant, ex = np.frexp(amax / 6.0)
        byte = np.where(mant > 0.5, ex, ex - 1) + 127
    byte = np.clip(np.where(amax > 0, byte, 1), 1, 254)
    scaled = (w * np.exp2(127.0 - byte)[:, None, :]).reshape(k, n).astype(np.float32)
    by_word = np.ascontiguousarray(scaled.reshape(k // 512, 128, 4, n).transpose(0, 1, 3, 2))
    if fmt == "e4m3":
        words = by_word.astype(ml_dtypes.float8_e4m3fn).view(np.uint8)
    else:
        c = by_word.astype(ml_dtypes.float4_e2m1fn).view(np.uint8) & 0xF
        words = (c[..., 0::2] | (c[..., 1::2] << 4)).reshape(k // 512, 128, 2 * n)
    return np.ascontiguousarray(words), np.ascontiguousarray(byte.astype(np.uint8).reshape(k // 512, 16, n))


def unpack_weight(words, scales, fmt):
    g, _, n = scales.shape
    words = np.ascontiguousarray(words).reshape(g, 128, n, -1)
    if fmt == "e4m3":
        vals = words.view(ml_dtypes.float8_e4m3fn).astype(np.float64)
    else:
        nib = np.empty((g, 128, n, 4), np.uint8)
        nib[..., 0::2] = words & 0xF
        nib[..., 1::2] = words >> 4
        vals = E2M1[nib]
    vals = vals * np.repeat(np.exp2(scales.astype(np.float64) - 127.0), 8, axis=1)[..., None]
    return vals.transpose(0, 1, 3, 2).reshape(g * 512, n)


K, T, J, R, N, E = 512, 1024, 256, 512, 256, 1024


def setup_inputs():
    n = np.random.standard_normal
    idx = np.random.permutation(T)[:J]
    idx2 = np.random.permutation(J)[:J]
    idx3 = np.random.permutation(J)[:J]
    idx4 = np.random.permutation(T)[:J]
    idx5 = np.random.permutation(E)[:J]
    fk = mx_kscale(K)
    fr = mx_kscale(R)
    xtp = pack_weight(n((K, T)) / fk[:, None], "e2m1")
    wp = pack_weight(n((K, R)) * 1 / np.sqrt(K) * fk[:, None] * fr, "e4m3")
    wbp = pack_weight(n((R, N)) * 1 / np.sqrt(R) / fr[:, None], "e2m1")
    wsp = pack_weight(n((K, N)) * 1 / np.sqrt(K) * fk[:, None], "e4m3")
    return {
        "xt_words": xtp[0],
        "xt_scales": xtp[1],
        "w_words": wp[0],
        "w_scales": wp[1],
        "wb_words": wbp[0],
        "wb_scales": wbp[1],
        "ws_words": wsp[0],
        "ws_scales": wsp[1],
        "offs": striped(idx),
        "offs2": striped(idx2),
        "offs3": striped(idx3),
        "offs4": striped(idx4),
        "offs5": striped(idx5),
    }


def reference(xt_words, xt_scales, w_words, w_scales, wb_words, wb_scales, ws_words, ws_scales, offs, offs2, offs3, offs4, offs5):
    idx = unstriped(offs)
    idx2 = unstriped(offs2)
    idx3 = unstriped(offs3)
    idx4 = unstriped(offs4)
    idx5 = unstriped(offs5)
    xtu = unpack_weight(xt_words, xt_scales, "e2m1")
    wu = unpack_weight(w_words, w_scales, "e4m3")
    wbu = unpack_weight(wb_words, wb_scales, "e2m1")
    wsu = unpack_weight(ws_words, ws_scales, "e4m3")
    xtidxg = xtu[:, idx]
    a = wu.T @ xtidxg
    h1 = np.maximum(a, a[:, idx2])
    hid = np.abs(h1 - h1[:, idx3])
    hidq = mxq(hid, 0, "e5m2")
    xtidx4g = xtu[:, idx4]
    p = wbu.T @ hidq + wsu.T @ xtidx4g
    y = np.zeros((N, E))
    y[:, idx5] = p
    return y

@@ -1,0 +1,157 @@
+from contextlib import ExitStack
+
+import concourse.mybir as mybir
+
+K, T, J, R, N, E = 512, 1024, 256, 512, 256, 1024
+FLOPS = 2 * J * (K * R + R * N + K * N)
+
+F32 = mybir.dt.float32
+BF16 = mybir.dt.bfloat16
+I32 = mybir.dt.int32
+U32 = mybir.dt.uint32
+U16 = mybir.dt.uint16
+U8 = mybir.dt.uint8
+E4M3 = mybir.dt.float8_e4m3fn_x4
+E5M2 = mybir.dt.float8_e5m2_x4
+E2M1 = mybir.dt.float4_e2m1fn_x4
+ALU = mybir.AluOpType
+ACT = mybir.ActivationFunctionType
+
+P = 128
+PACK = 4
+WIN = 2 * J
+
+
+def tile_list_passedon_solo_further_scattered_kernel(
+    tc, xt_words, xt_scales, w_words, w_scales, wb_words, wb_scales, ws_words, ws_scales,
+    offs, offs2, offs3, offs4, offs5, out,
+):
+    nc = tc.nc
+    with ExitStack() as ctx:
+        lists = ctx.enter_context(tc.tile_pool(name="lists", bufs=1))
+        sb = ctx.enter_context(tc.tile_pool(name="sb", bufs=1))
+        psum = ctx.enter_context(tc.psum_pool(name="psum", bufs=1))
+
+        def load_list(src, name):
+            t = lists.tile([P, J // 16], U16, name=name)
+            nc.sync.dma_start(t[:], src)
+            return t
+
+        def load_scales(plane, src, quads):
+            for q in quads:
+                nc.sync.dma_start(plane[32 * q : 32 * q + 4, :].bitcast(I32), src[0, 4 * q : 4 * q + 4, :].bitcast(I32))
+
+        xs = sb.tile([P, T], U8, name="xs", align_bytes=64)
+        w_sc = sb.tile([P, R], U8, name="w_sc", tag="w_sc_x4", align_bytes=64)
+        ws_sc = sb.tile([P, N], U8, name="ws_sc", align_bytes=64)
+        wb_sc = sb.tile([P, N], U8, name="wb_sc", align_bytes=64)
+        nc.vector.memset(xs[:].bitcast(I32), 0)
+        nc.gpsimd.memset(w_sc[:].bitcast(I32), 0)
+        nc.gpsimd.memset(ws_sc[:].bitcast(I32), 0)
+        nc.gpsimd.memset(wb_sc[:].bitcast(I32), 0)
+
+        xw = sb.tile([P, T], U16, name="xw", align_bytes=64)
+        w_raw = sb.tile([P, R], U32, name="w_raw", tag="weights", align_bytes=64)
+
+        l1 = load_list(offs, "l1")
+        l2 = load_list(offs2, "l2")
+        l3 = load_list(offs3, "l3")
+        l4 = load_list(offs4, "l4")
+        l5 = load_list(offs5, "l5")
+        load_scales(xs, xt_scales, range(0, 1))
+        nc.sync.dma_start(xw[:].bitcast(I32), xt_words[0].bitcast(I32))
+        nc.sync.dma_start(w_raw[:].bitcast(I32), w_words[0].rearrange("p n t -> p (n t)").bitcast(I32))
+        load_scales(xs, xt_scales, range(1, 4))
+        load_scales(w_sc, w_scales, range(4))
+        load_scales(ws_sc, ws_scales, range(4))
+        load_scales(wb_sc, wb_scales, range(4))
+
+        pages = [sb.tile([P, E], F32, name="page%d" % h) for h in range(2)]
+        for h in range(2):
+            nc.vector.memset(pages[h][:], 0.0)
+
+        xg_s = sb.tile([P, J], U8, name="xg_s", align_bytes=64)
+        xg_w = sb.tile([P, J], U16, name="xg_w", align_bytes=64)
+        nc.vector.tensor_copy(xg_w[:], xw[:].indirect(l1[:]))
+        nc.vector.tensor_copy(xg_s[:], xs[:].indirect(l1[:]))
+
+        w_perm = sb.tile([P, R], U32, name="w_perm", align_bytes=64)
+        w_sc_perm = sb.tile([P, R], U8, name="w_sc_perm", align_bytes=64)
+        nc.vector.tensor_copy(w_perm[:].rearrange("p (t m) -> p m t", t=PACK), w_raw[:].rearrange("p (m t) -> p m t", t=PACK))
+        for u in range(0, PACK, 2):
+            nc.vector.tensor_copy(
+                w_sc_perm[:].rearrange("p (t m) -> p t m", t=PACK)[:, u : u + 2, :],
+                w_sc[:].rearrange("p (m t) -> p t m", t=PACK)[:, u : u + 2, :],
+            )
+
+        late = sb.tile([P, N + N // 2], U32, name="late", tag="weights", align_bytes=64)
+        ws_w = late[:, 0:N]
+        wb_w = late[:, N : N + N // 2].bitcast(U8)
+        nc.sync.dma_start(ws_w.bitcast(I32), ws_words[0].rearrange("p n t -> p (n t)").bitcast(I32))
+        nc.sync.dma_start(wb_w.bitcast(I32), wb_words[0].bitcast(I32))
+
+        a_ps = [psum.tile([P, J], F32, name="a_ps%d" % t) for t in range(PACK)]
+        for t in range(PACK):
+            cols = slice(P * t, P * (t + 1))
+            nc.tensor.matmul_mx(
+                out=a_ps[t][:], lhsT=w_perm[:, cols].bitcast(E4M3), lhsT_scale=w_sc_perm[:, cols],
+                rhs=xg_w[:].bitcast(E2M1), rhs_scale=xg_s[:], start=True, stop=True,
+            )
+
+        x4_w = sb.tile([P, J], U16, name="x4_w", tag="w_sc_x4", align_bytes=64)
+        nc.vector.tensor_copy(x4_w[:], xw[:].indirect(l4[:]))
+
+        def move(on_vector, dst, src):
+            if on_vector:
+                nc.vector.tensor_copy(dst, src)
+            else:
+                nc.scalar.activation(dst, src, ACT.Copy)
+
+        a_sb = [sb.tile([P, WIN], F32, name="a_sb%d" % t) for t in range(PACK)]
+        g2 = [sb.tile([P, J], F32, name="g2_%d" % t) for t in range(PACK)]
+        h1 = sb.tile([P, PACK, J], F32, name="h1")
+        for t in range(PACK):
+            move(t in (0, 2), a_sb[t][:, 0:J], a_ps[t][:])
+        for t in range(PACK):
+            move(t in (0, 2), g2[t][:], a_sb[t][:].indirect(l2[:]))
+        for t in range(PACK):
+            nc.vector.tensor_tensor(h1[:, t, :], a_sb[t][:, 0:J], g2[t][:], ALU.max)
+
+        NP = 2
+        JP = J // NP
+        js = [slice(JP * s, JP * (s + 1)) for s in range(NP)]
+        ls = [slice(JP // 16 * s, JP // 16 * (s + 1)) for s in range(NP)]
+        g3 = [sb.tile([P, PACK, JP], F32, name="g3_%d" % s, align_bytes=64) for s in range(NP)]
+        for s in range(NP):
+            for t in range(PACK):
+                move((s, t) in ((1, 0), (1, 1), (1, 2)), g3[s][:, t, :], h1[:, t, :].indirect(l3[:, ls[s]]))
+        d = [sb.tile([P, PACK, JP], F32, name="d%d" % s) for s in range(NP)]
+        for s in range(NP):
+            nc.vector.tensor_tensor(d[s][:], h1[:, :, js[s]], g3[s][:], ALU.subtract)
+        x4_s = sb.tile([P, J], U8, name="x4_s", tag="g3_0", align_bytes=64)
+        nc.vector.tensor_copy(x4_s[:], xs[:].indirect(l4[:]))
+        for s in range(NP):
+            hid = sb.tile([P, JP, PACK], BF16, name="hid%d" % s, align_bytes=64)
+            hq_w = sb.tile([P, JP], U32, name="hq_w%d" % s, align_bytes=64)
+            hq_s = sb.tile([P, JP], U8, name="hq_s%d" % s, align_bytes=64)
+            nc.scalar.activation(
+                hid[:].rearrange("p (c i) t -> p c t i", i=4),
+                d[s][:].rearrange("p t (c i) -> p c t i", i=4), ACT.Abs,
+            )
+            nc.vector.quantize_mx(out=hq_w[:].bitcast(E5M2), scales=hq_s[:], in_=hid[:].rearrange("p j t -> p (j t)"))
+            for h in range(2):
+                p_ps = psum.tile([P, JP], F32, name="p_ps%d_%d" % (s, h))
+                cols = slice(P * h, P * (h + 1))
+                nc.tensor.matmul_mx(
+                    out=p_ps[:], lhsT=ws_w[:, cols].bitcast(E4M3), lhsT_scale=ws_sc[:, cols],
+                    rhs=x4_w[:, js[s]].bitcast(E2M1), rhs_scale=x4_s[:, js[s]], start=True, stop=False,
+                )
+                nc.tensor.matmul_mx(
+                    out=p_ps[:], lhsT=wb_w[:, 2 * P * h : 2 * P * (h + 1)].bitcast(E2M1), lhsT_scale=wb_sc[:, cols],
+                    rhs=hq_w[:].bitcast(E5M2), rhs_scale=hq_s[:], start=False, stop=True,
+                )
+                p_sb = sb.tile([P, JP], F32, name="p_sb%d_%d" % (s, h))
+                move(h == 0, p_sb[:], p_ps[:])
+                move(h == 0, pages[h][:].indirect(l5[:, ls[s]]), p_sb[:])
+        for h in range(2):
+            nc.sync.dma_start(out[P * h : P * (h + 1), :], pages[h][:])

@@ -54,21 +54,20 @@ def tile_list_passedon_solo_further_scattered_kernel(
         w_raw = sb.tile([P, R], U32, name="w_raw", tag="weights", align_bytes=64)
 
         l1 = load_list(offs, "l1")
-        l2 = load_list(offs2, "l2")
-        l3 = load_list(offs3, "l3")
-        l4 = load_list(offs4, "l4")
-        l5 = load_list(offs5, "l5")
-        load_scales(xs, xt_scales, range(0, 1))
         nc.sync.dma_start(xw[:].bitcast(I32), xt_words[0].bitcast(I32))
+        load_scales(xs, xt_scales, range(4))
         nc.sync.dma_start(w_raw[:].bitcast(I32), w_words[0].rearrange("p n t -> p (n t)").bitcast(I32))
-        load_scales(xs, xt_scales, range(1, 4))
         load_scales(w_sc, w_scales, range(4))
+        l2 = load_list(offs2, "l2")
+        l4 = load_list(offs4, "l4")
+        l3 = load_list(offs3, "l3")
         load_scales(ws_sc, ws_scales, range(4))
         load_scales(wb_sc, wb_scales, range(4))
+        l5 = load_list(offs5, "l5")
 
         pages = [sb.tile([P, E], F32, name="page%d" % h) for h in range(2)]
         for h in range(2):
-            nc.vector.memset(pages[h][:], 0.0)
+            nc.vector.memset(pages[h][:].bitcast(I32), 0)
 
         xg_s = sb.tile([P, J], U8, name="xg_s", align_bytes=64)
         xg_w = sb.tile([P, J], U16, name="xg_w", align_bytes=64)
@@ -98,8 +97,10 @@ def tile_list_passedon_solo_further_scattered_kernel(
                 rhs=xg_w[:].bitcast(E2M1), rhs_scale=xg_s[:], start=True, stop=True,
             )
 
+        x4_s = sb.tile([P, J], U8, name="x4_s", align_bytes=64)
         x4_w = sb.tile([P, J], U16, name="x4_w", tag="w_sc_x4", align_bytes=64)
         nc.vector.tensor_copy(x4_w[:], xw[:].indirect(l4[:]))
+        nc.vector.tensor_copy(x4_s[:], xs[:].indirect(l4[:]))
 
         def move(on_vector, dst, src):
             if on_vector:
@@ -111,9 +112,9 @@ def tile_list_passedon_solo_further_scattered_kernel(
         g2 = [sb.tile([P, J], F32, name="g2_%d" % t) for t in range(PACK)]
         h1 = sb.tile([P, PACK, J], F32, name="h1")
         for t in range(PACK):
-            move(t in (0, 2), a_sb[t][:, 0:J], a_ps[t][:])
+            move(t in (), a_sb[t][:, 0:J], a_ps[t][:])
         for t in range(PACK):
-            move(t in (0, 2), g2[t][:], a_sb[t][:].indirect(l2[:]))
+            move(t in (0, 1), g2[t][:], a_sb[t][:].indirect(l2[:]))
         for t in range(PACK):
             nc.vector.tensor_tensor(h1[:, t, :], a_sb[t][:, 0:J], g2[t][:], ALU.max)
 
@@ -121,15 +122,14 @@ def tile_list_passedon_solo_further_scattered_kernel(
         JP = J // NP
         js = [slice(JP * s, JP * (s + 1)) for s in range(NP)]
         ls = [slice(JP // 16 * s, JP // 16 * (s + 1)) for s in range(NP)]
-        g3 = [sb.tile([P, PACK, JP], F32, name="g3_%d" % s, align_bytes=64) for s in range(NP)]
+        g3 = [sb.tile([P, PACK, JP], F32, name="g3_%d" % s) for s in range(NP)]
         for s in range(NP):
             for t in range(PACK):
-                move((s, t) in ((1, 0), (1, 1), (1, 2)), g3[s][:, t, :], h1[:, t, :].indirect(l3[:, ls[s]]))
+                move((s, t) in ((0, 2), (0, 3)), g3[s][:, t, :], h1[:, t, :].indirect(l3[:, ls[s]]))
         d = [sb.tile([P, PACK, JP], F32, name="d%d" % s) for s in range(NP)]
         for s in range(NP):
             nc.vector.tensor_tensor(d[s][:], h1[:, :, js[s]], g3[s][:], ALU.subtract)
-        x4_s = sb.tile([P, J], U8, name="x4_s", tag="g3_0", align_bytes=64)
-        nc.vector.tensor_copy(x4_s[:], xs[:].indirect(l4[:]))
+        p_sb = [sb.tile([P, J], F32, name="p_sb%d" % h) for h in range(2)]
         for s in range(NP):
             hid = sb.tile([P, JP, PACK], BF16, name="hid%d" % s, align_bytes=64)
             hq_w = sb.tile([P, JP], U32, name="hq_w%d" % s, align_bytes=64)
@@ -150,8 +150,8 @@ def tile_list_passedon_solo_further_scattered_kernel(
                     out=p_ps[:], lhsT=wb_w[:, 2 * P * h : 2 * P * (h + 1)].bitcast(E2M1), lhsT_scale=wb_sc[:, cols],
                     rhs=hq_w[:].bitcast(E5M2), rhs_scale=hq_s[:], start=False, stop=True,
                 )
-                p_sb = sb.tile([P, JP], F32, name="p_sb%d_%d" % (s, h))
-                move(h == 0, p_sb[:], p_ps[:])
-                move(h == 0, pages[h][:].indirect(l5[:, ls[s]]), p_sb[:])
+                move((s, h) != (0, 0), p_sb[h][:, js[s]], p_ps[:])
+            move(s == 1, pages[0][:].indirect(l5[:, ls[s]]), p_sb[0][:, js[s]])
+        move(False, pages[1][:].indirect(l5[:]), p_sb[1][:])
         for h in range(2):
             nc.sync.dma_start(out[P * h : P * (h + 1), :], pages[h][:])

@@ -77,10 +77,10 @@ def tile_list_passedon_solo_further_scattered_kernel(
         w_perm = sb.tile([P, R], U32, name="w_perm", align_bytes=64)
         w_sc_perm = sb.tile([P, R], U8, name="w_sc_perm", align_bytes=64)
         nc.vector.tensor_copy(w_perm[:].rearrange("p (t m) -> p m t", t=PACK), w_raw[:].rearrange("p (m t) -> p m t", t=PACK))
-        for u in range(0, PACK, 2):
+        for u in range(PACK):
             nc.vector.tensor_copy(
-                w_sc_perm[:].rearrange("p (t m) -> p t m", t=PACK)[:, u : u + 2, :],
-                w_sc[:].rearrange("p (m t) -> p t m", t=PACK)[:, u : u + 2, :],
+                w_sc_perm[:].rearrange("p (t m) -> p t m", t=PACK)[:, u : u + 1, :],
+                w_sc[:].rearrange("p (m t) -> p t m", t=PACK)[:, u : u + 1, :],
             )
 
         late = sb.tile([P, N + N // 2], U32, name="late", tag="weights", align_bytes=64)
@@ -127,8 +127,8 @@ def tile_list_passedon_solo_further_scattered_kernel(
             for t in range(PACK):
                 move((s, t) in ((0, 2), (0, 3)), g3[s][:, t, :], h1[:, t, :].indirect(l3[:, ls[s]]))
         d = [sb.tile([P, PACK, JP], F32, name="d%d" % s) for s in range(NP)]
-        for s in range(NP):
-            nc.vector.tensor_tensor(d[s][:], h1[:, :, js[s]], g3[s][:], ALU.subtract)
+        for s, ts in ((0, slice(0, 3)), (0, slice(3, 4)), (1, slice(0, 3)), (1, slice(3, 4))):
+            nc.vector.tensor_tensor(d[s][:, ts, :], h1[:, ts, js[s]], g3[s][:, ts, :], ALU.subtract)
         p_sb = [sb.tile([P, J], F32, name="p_sb%d" % h) for h in range(2)]
         for s in range(NP):
             hid = sb.tile([P, JP, PACK], BF16, name="hid%d" % s, align_bytes=64)

from contextlib import ExitStack

import concourse.mybir as mybir

K, T, J, R, N, E = 512, 1024, 256, 512, 256, 1024
FLOPS = 2 * J * (K * R + R * N + K * N)

F32 = mybir.dt.float32
BF16 = mybir.dt.bfloat16
I32 = mybir.dt.int32
U32 = mybir.dt.uint32
U16 = mybir.dt.uint16
U8 = mybir.dt.uint8
E4M3 = mybir.dt.float8_e4m3fn_x4
E5M2 = mybir.dt.float8_e5m2_x4
E2M1 = mybir.dt.float4_e2m1fn_x4
ALU = mybir.AluOpType
ACT = mybir.ActivationFunctionType

P = 128
PACK = 4
WIN = 2 * J


def tile_list_passedon_solo_further_scattered_kernel(
    tc, xt_words, xt_scales, w_words, w_scales, wb_words, wb_scales, ws_words, ws_scales,
    offs, offs2, offs3, offs4, offs5, out,
):
    nc = tc.nc
    with ExitStack() as ctx:
        lists = ctx.enter_context(tc.tile_pool(name="lists", bufs=1))
        sb = ctx.enter_context(tc.tile_pool(name="sb", bufs=1))
        psum = ctx.enter_context(tc.psum_pool(name="psum", bufs=1))

        def load_list(src, name):
            t = lists.tile([P, J // 16], U16, name=name)
            nc.sync.dma_start(t[:], src)
            return t

        def load_scales(plane, src, quads):
            for q in quads:
                nc.sync.dma_start(plane[32 * q : 32 * q + 4, :].bitcast(I32), src[0, 4 * q : 4 * q + 4, :].bitcast(I32))

        xs = sb.tile([P, T], U8, name="xs", align_bytes=64)
        w_sc = sb.tile([P, R], U8, name="w_sc", tag="w_sc_x4", align_bytes=64)
        ws_sc = sb.tile([P, N], U8, name="ws_sc", align_bytes=64)
        wb_sc = sb.tile([P, N], U8, name="wb_sc", align_bytes=64)
        nc.vector.memset(xs[:].bitcast(I32), 0)
        nc.gpsimd.memset(w_sc[:].bitcast(I32), 0)
        nc.gpsimd.memset(ws_sc[:].bitcast(I32), 0)
        nc.gpsimd.memset(wb_sc[:].bitcast(I32), 0)

        xw = sb.tile([P, T], U16, name="xw", align_bytes=64)
        w_raw = sb.tile([P, R], U32, name="w_raw", tag="weights", align_bytes=64)

        l1 = load_list(offs, "l1")
        nc.sync.dma_start(xw[:].bitcast(I32), xt_words[0].bitcast(I32))
        load_scales(xs, xt_scales, range(4))
        nc.sync.dma_start(w_raw[:].bitcast(I32), w_words[0].rearrange("p n t -> p (n t)").bitcast(I32))
        load_scales(w_sc, w_scales, range(4))
        l2 = load_list(offs2, "l2")
        l4 = load_list(offs4, "l4")
        l3 = load_list(offs3, "l3")
        load_scales(ws_sc, ws_scales, range(4))
        load_scales(wb_sc, wb_scales, range(4))
        l5 = load_list(offs5, "l5")

        pages = [sb.tile([P, E], F32, name="page%d" % h) for h in range(2)]
        for h in range(2):
            nc.vector.memset(pages[h][:].bitcast(I32), 0)

        xg_s = sb.tile([P, J], U8, name="xg_s", align_bytes=64)
        xg_w = sb.tile([P, J], U16, name="xg_w", align_bytes=64)
        nc.vector.tensor_copy(xg_w[:], xw[:].indirect(l1[:]))
        nc.vector.tensor_copy(xg_s[:], xs[:].indirect(l1[:]))

        w_perm = sb.tile([P, R], U32, name="w_perm", align_bytes=64)
        w_sc_perm = sb.tile([P, R], U8, name="w_sc_perm", align_bytes=64)
        nc.vector.tensor_copy(w_perm[:].rearrange("p (t m) -> p m t", t=PACK), w_raw[:].rearrange("p (m t) -> p m t", t=PACK))
        for u in range(PACK):
            nc.vector.tensor_copy(
                w_sc_perm[:].rearrange("p (t m) -> p t m", t=PACK)[:, u : u + 1, :],
                w_sc[:].rearrange("p (m t) -> p t m", t=PACK)[:, u : u + 1, :],
            )

        late = sb.tile([P, N + N // 2], U32, name="late", tag="weights", align_bytes=64)
        ws_w = late[:, 0:N]
        wb_w = late[:, N : N + N // 2].bitcast(U8)
        nc.sync.dma_start(ws_w.bitcast(I32), ws_words[0].rearrange("p n t -> p (n t)").bitcast(I32))
        nc.sync.dma_start(wb_w.bitcast(I32), wb_words[0].bitcast(I32))

        a_ps = [psum.tile([P, J], F32, name="a_ps%d" % t) for t in range(PACK)]
        for t in range(PACK):
            cols = slice(P * t, P * (t + 1))
            nc.tensor.matmul_mx(
                out=a_ps[t][:], lhsT=w_perm[:, cols].bitcast(E4M3), lhsT_scale=w_sc_perm[:, cols],
                rhs=xg_w[:].bitcast(E2M1), rhs_scale=xg_s[:], start=True, stop=True,
            )

        x4_s = sb.tile([P, J], U8, name="x4_s", align_bytes=64)
        x4_w = sb.tile([P, J], U16, name="x4_w", tag="w_sc_x4", align_bytes=64)
        nc.vector.tensor_copy(x4_w[:], xw[:].indirect(l4[:]))
        nc.vector.tensor_copy(x4_s[:], xs[:].indirect(l4[:]))

        def move(on_vector, dst, src):
            if on_vector:
                nc.vector.tensor_copy(dst, src)
            else:
                nc.scalar.activation(dst, src, ACT.Copy)

        a_sb = [sb.tile([P, WIN], F32, name="a_sb%d" % t) for t in range(PACK)]
        g2 = [sb.tile([P, J], F32, name="g2_%d" % t) for t in range(PACK)]
        h1 = sb.tile([P, PACK, J], F32, name="h1")
        for t in range(PACK):
            move(t in (), a_sb[t][:, 0:J], a_ps[t][:])
        for t in range(PACK):
            move(t in (0, 1), g2[t][:], a_sb[t][:].indirect(l2[:]))
        for t in range(PACK):
            nc.vector.tensor_tensor(h1[:, t, :], a_sb[t][:, 0:J], g2[t][:], ALU.max)

        NP = 2
        JP = J // NP
        js = [slice(JP * s, JP * (s + 1)) for s in range(NP)]
        ls = [slice(JP // 16 * s, JP // 16 * (s + 1)) for s in range(NP)]
        g3 = [sb.tile([P, PACK, JP], F32, name="g3_%d" % s) for s in range(NP)]
        for s in range(NP):
            for t in range(PACK):
                move((s, t) in ((0, 2), (0, 3)), g3[s][:, t, :], h1[:, t, :].indirect(l3[:, ls[s]]))
        d = [sb.tile([P, PACK, JP], F32, name="d%d" % s) for s in range(NP)]
        for s, ts in ((0, slice(0, 3)), (0, slice(3, 4)), (1, slice(0, 3)), (1, slice(3, 4))):
            nc.vector.tensor_tensor(d[s][:, ts, :], h1[:, ts, js[s]], g3[s][:, ts, :], ALU.subtract)
        p_sb = [sb.tile([P, J], F32, name="p_sb%d" % h) for h in range(2)]
        for s in range(NP):
            hid = sb.tile([P, JP, PACK], BF16, name="hid%d" % s, align_bytes=64)
            hq_w = sb.tile([P, JP], U32, name="hq_w%d" % s, align_bytes=64)
            hq_s = sb.tile([P, JP], U8, name="hq_s%d" % s, align_bytes=64)
            nc.scalar.activation(
                hid[:].rearrange("p (c i) t -> p c t i", i=4),
                d[s][:].rearrange("p t (c i) -> p c t i", i=4), ACT.Abs,
            )
            nc.vector.quantize_mx(out=hq_w[:].bitcast(E5M2), scales=hq_s[:], in_=hid[:].rearrange("p j t -> p (j t)"))
            for h in range(2):
                p_ps = psum.tile([P, JP], F32, name="p_ps%d_%d" % (s, h))
                cols = slice(P * h, P * (h + 1))
                nc.tensor.matmul_mx(
                    out=p_ps[:], lhsT=ws_w[:, cols].bitcast(E4M3), lhsT_scale=ws_sc[:, cols],
                    rhs=x4_w[:, js[s]].bitcast(E2M1), rhs_scale=x4_s[:, js[s]], start=True, stop=False,
                )
                nc.tensor.matmul_mx(
                    out=p_ps[:], lhsT=wb_w[:, 2 * P * h : 2 * P * (h + 1)].bitcast(E2M1), lhsT_scale=wb_sc[:, cols],
                    rhs=hq_w[:].bitcast(E5M2), rhs_scale=hq_s[:], start=False, stop=True,
                )
                move((s, h) != (0, 0), p_sb[h][:, js[s]], p_ps[:])
            move(s == 1, pages[0][:].indirect(l5[:, ls[s]]), p_sb[0][:, js[s]])
        move(False, pages[1][:].indirect(l5[:]), p_sb[1][:])
        for h in range(2):
            nc.sync.dma_start(out[P * h : P * (h + 1), :], pages[h][:])
